import numpy as np
import ml_dtypes


def mxq(x, axis, fmt="e4m3"):
    dtype, down = {"e4m3": (ml_dtypes.float8_e4m3fn, 7), "e5m2": (ml_dtypes.float8_e5m2, 14)}[fmt]
    v = np.moveaxis(np.asarray(x, np.float32).astype(ml_dtypes.bfloat16).astype(np.float64), axis, -1)
    blocks = v.reshape(v.shape[:-1] + (-1, 32))
    amax = np.abs(blocks).max(-1, keepdims=True)
    byte = np.maximum(np.where(amax > 0, np.frexp(amax)[1] - 1 + 127, 0) - down, 1)
    scale = np.exp2(byte - 127.0)
    codes = (blocks / scale).astype(np.float32).astype(dtype).astype(np.float64)
    return np.moveaxis((codes * scale).reshape(v.shape), -1, axis)


WIDE = False


def mx_kscale(k):
    if not WIDE:
        return np.ones(k)
    levels = np.array([10, -10, 5, -5, 0])
    if k % 512:
        return np.exp2(np.random.permutation(np.resize(levels, k // 32))).repeat(32)
    a = np.empty((k // 512, 16))
    for p in range(k // 512):
        a[p, :8] = np.random.permutation(np.resize(levels, 8))
        for g in range(8):
            far = levels[np.abs(levels - a[p, g]) >= 10]
            a[p, g + 8] = far[np.random.randint(len(far))]
    return np.exp2(a.ravel()).repeat(32)


def f64(x):
    return np.asarray(x).astype(np.float64)


def striped(idx):
    return np.tile(idx.reshape(-1, 16).T, (8, 1)).astype(np.uint16)


def unstriped(offs):
    return offs[:16].T.reshape(-1).astype(np.int64)


E2M1 = np.array([0.0, 0.5, 1.0, 1.5, 2.0, 3.0, 4.0, 6.0, -0.0, -0.5, -1.0, -1.5, -2.0, -3.0, -4.0, -6.0])


def pack_weight(w, fmt):
    k, n = w.shape
    w = f64(np.asarray(w, np.float32).astype(ml_dtypes.bfloat16)).reshape(k // 32, 32, n)
    amax = np.abs(w).max(1)
    if fmt == "e4m3":
        byte = np.frexp(amax)[1] - 1 + 127 - 7
    else:
        mant, ex = np.frexp(amax / 6.0)
        byte = np.where(mant > 0.5, ex, ex - 1) + 127
    byte = np.clip(np.where(amax > 0, byte, 1), 1, 254)
    scaled = (w * np.exp2(127.0 - byte)[:, None, :]).reshape(k, n).astype(np.float32)
    by_word = np.ascontiguousarray(scaled.reshape(k // 512, 128, 4, n).transpose(0, 1, 3, 2))
    if fmt == "e4m3":
        words = by_word.astype(ml_dtypes.float8_e4m3fn).view(np.uint8)
    else:
        c = by_word.astype(ml_dtypes.float4_e2m1fn).view(np.uint8) & 0xF
        words = (c[..., 0::2] | (c[..., 1::2] << 4)).reshape(k // 512, 128, 2 * n)
    return np.ascontiguousarray(words), np.ascontiguousarray(byte.astype(np.uint8).reshape(k // 512, 16, n))


def unpack_weight(words, scales, fmt):
    g, _, n = scales.shape
    words = np.ascontiguousarray(words).reshape(g, 128, n, -1)
    if fmt == "e4m3":
        vals = words.view(ml_dtypes.float8_e4m3fn).astype(np.float64)
    else:
        nib = np.empty((g, 128, n, 4), np.uint8)
        nib[..., 0::2] = words & 0xF
        nib[..., 1::2] = words >> 4
        vals = E2M1[nib]
    vals = vals * np.repeat(np.exp2(scales.astype(np.float64) - 127.0), 8, axis=1)[..., None]
    return vals.transpose(0, 1, 3, 2).reshape(g * 512, n)


def relu(v):
    return np.maximum(v, 0.0)


K, T, E, C, N = 1024, 2048, 24, 128, 256
R = 2


def by_expert(wq, xq):
    return np.concatenate([wq[e].T @ xq[:, e * C:(e + 1) * C] for e in range(E)], axis=1)


def setup_inputs():
    n = np.random.standard_normal
    s = mx_kscale(K)[:, None]
    slot_token = np.concatenate([r * (T // R) + np.random.permutation(T // R)[:C // R] for e in range(E) for r in range(R)])
    x = pack_weight(n((K, T)) * s, "e4m3")
    return {
        "x_words": x[0],
        "x_scales": x[1],
        "w": (n((E, K, N)) / np.sqrt(K) / s[None]).astype(np.float32),
        "b": (0.3 * n((N, E))).astype(np.float32),
        "offs": striped(slot_token),
    }


def reference(x_words, x_scales, w, b, offs):
    idx = unstriped(offs)
    xq = unpack_weight(x_words, x_scales, "e4m3")[:, idx]
    y = by_expert(mxq(f64(w), 1, "e4m3"), xq)
    y = relu(y + np.repeat(f64(b), C, axis=1))
    return y.reshape(N, E, R, C // R).transpose(0, 2, 1, 3).reshape(N, E * C)

@@ -1,0 +1,142 @@
+from contextlib import ExitStack
+
+import concourse.mybir as mybir
+
+K, T, E, C, N = 1024, 2048, 24, 128, 256
+R = 2
+FLOPS = 2 * K * N * E * C
+
+F32 = mybir.dt.float32
+BF16 = mybir.dt.bfloat16
+I32 = mybir.dt.int32
+U32 = mybir.dt.uint32
+U16 = mybir.dt.uint16
+U8 = mybir.dt.uint8
+FP8X4 = mybir.dt.float8_e4m3fn_x4
+RELU = mybir.ActivationFunctionType.Relu
+
+P = 128
+PACK = 4
+PASSES = K // (P * PACK)
+HALVES = N // P
+PER_RANK = C // R
+GATHER_EXPERTS = 3
+FIRST_GATHER = (5, 3, 4)
+GATHER_LEAD = 3
+RING = 7
+SCALAR_COLS = 96
+STORE_EDGES = (0, 18, 22, 24)
+
+
+def tile_moe_pke_lin_relu_kernel(tc, x_words, x_scales, w, b, offs, out):
+    nc = tc.nc
+    with ExitStack() as ctx:
+        keep = ctx.enter_context(tc.tile_pool(name="keep", bufs=1))
+        raw_pool = ctx.enter_context(tc.tile_pool(name="raw", bufs=12))
+        ring = ctx.enter_context(tc.tile_pool(name="ring", bufs=1))
+        code_pool = ctx.enter_context(tc.tile_pool(name="code", bufs=4))
+        psum = ctx.enter_context(tc.psum_pool(name="psum", bufs=4))
+
+        offsets = keep.tile([P, E * C // 16], U16, name="offsets")
+        nc.sync.dma_start(offsets[:], offs)
+
+        scale_rows = keep.tile([P, T // 4], I32, name="scale_rows")
+        token_scales = keep.tile([P, T], U8, name="token_scales", align_bytes=64)
+        nc.vector.memset(token_scales[:].bitcast(I32), 0)
+        for q in range(4):
+            live = slice(32 * q, 32 * q + 4 * PASSES)
+            nc.sync.dma_start(scale_rows[live, :], x_scales[:, 4 * q : 4 * q + 4, :].bitcast(I32))
+            nc.vector.tensor_copy(token_scales[live, :].bitcast(I32), scale_rows[live, :])
+        token_words = []
+        for o in range(PASSES):
+            words = keep.tile([P, T], U32, name="token_words%d" % o, align_bytes=64)
+            nc.sync.dma_start(words[:].bitcast(I32), x_words[o].rearrange("p t r -> p (t r)").bitcast(I32))
+            token_words.append(words)
+        bias = keep.tile([P, HALVES, E], F32, name="bias")
+        nc.sync.dma_start(bias[:], b.rearrange("(h p) e -> p h e", p=P))
+
+        results = {}
+        for e0, e1 in zip(STORE_EDGES[:-1], STORE_EDGES[1:]):
+            for h in range(HALVES):
+                results[e0, h] = keep.tile([P, R, (e1 - e0) * PER_RANK], F32, name="result%d_%d" % (e0, h))
+
+        windows = token_words + [token_scales]
+        gather_edges = [[0] + list(range(first, E - 1, GATHER_EXPERTS)) + [E] for first in FIRST_GATHER]
+        slots = [[] for window in windows]
+
+        def gather(table, e0, tag):
+            edges = gather_edges[table]
+            e1 = edges[edges.index(e0) + 1]
+            dtype = U8 if table == PASSES else U32
+            picked = ring.tile([P, (e1 - e0) * C], dtype, name="picked", tag=tag, align_bytes=64)
+            nc.vector.tensor_copy(picked[:], windows[table][:].indirect(offsets[:, e0 * C // 16 : e1 * C // 16]))
+            slots[table].extend(picked[:, (e - e0) * C : (e - e0 + 1) * C] for e in range(e0, e1))
+
+        rounded_of = {}
+
+        def load_and_cast(e):
+            raw = raw_pool.tile([P, PASSES, PACK, N], F32, name="raw")
+            nc.sync.dma_start(raw[:], w[e].rearrange("(o p j) n -> p o j n", p=P, j=PACK))
+            rounded = ring.tile([P, PASSES, N, PACK], BF16, name="rounded", tag="ring%d" % (e % RING), align_bytes=64)
+            rounded_of[e] = rounded
+
+            def views(o, n0, n1):
+                return (
+                    rounded[:, o, n0:n1, :].rearrange("p (c i) j -> p c j i", i=4),
+                    raw[:, o, :, n0:n1].rearrange("p j (c i) -> p c j i", i=4),
+                )
+
+            nc.scalar.copy(*views(0, 0, N))
+            nc.scalar.copy(*views(1, 0, SCALAR_COLS))
+            nc.vector.tensor_copy(*views(1, SCALAR_COLS, N))
+
+        def quantize(e):
+            codes = code_pool.tile([P, PASSES * N], U32, name="codes", align_bytes=64)
+            scales = code_pool.tile([P, PASSES * N], U8, name="scales", align_bytes=64)
+            nc.vector.quantize_mx(
+                out=codes[:].bitcast(FP8X4),
+                scales=scales[:],
+                in_=rounded_of[e][:].rearrange("p o n j -> p (o n j)"),
+            )
+            return codes, scales
+
+        def multiply(e, codes, scales):
+            acc = psum.tile([P, HALVES, C], F32, name="acc")
+            for h in range(HALVES):
+                for o in range(PASSES):
+                    cols = slice(o * N + h * P, o * N + (h + 1) * P)
+                    nc.tensor.matmul_mx(
+                        out=acc[:, h, :],
+                        lhsT=codes[:, cols].bitcast(FP8X4),
+                        lhsT_scale=scales[:, cols],
+                        rhs=slots[o][e].bitcast(FP8X4),
+                        rhs_scale=slots[PASSES][e][4 * o : P, :],
+                        start=(o == 0),
+                        stop=(o == PASSES - 1),
+                    )
+            e0 = max(edge for edge in STORE_EDGES if edge <= e)
+            for h in range(HALVES):
+                nc.scalar.activation(
+                    results[e0, h][:, :, (e - e0) * PER_RANK : (e - e0 + 1) * PER_RANK],
+                    acc[:, h, :].rearrange("p (m u) -> p m u", m=R),
+                    RELU,
+                    bias=bias[:, h, e : e + 1],
+                )
+
+        for table in (0, 2, 1):
+            gather(table, 0, "ring%d" % (FIRST_GATHER[table] + 1))
+        for step in range(E + 1):
+            if step < E:
+                load_and_cast(step)
+            if step >= 1:
+                e = step - 1
+                codes, scales = quantize(e)
+                for table, edges in enumerate(gather_edges):
+                    if e + GATHER_LEAD in edges[:-1]:
+                        gather(table, e + GATHER_LEAD, "ring%d" % (e % RING))
+                multiply(e, codes, scales)
+
+        for e0, e1 in zip(STORE_EDGES[:-1], STORE_EDGES[1:]):
+            for h in range(HALVES):
+                rows = out[h * P : (h + 1) * P, :].rearrange("p (m c) -> p m c", m=R)
+                nc.sync.dma_start(rows[:, :, e0 * PER_RANK : e1 * PER_RANK], results[e0, h][:])

@@ -21,10 +21,10 @@ PASSES = K // (P * PACK)
 HALVES = N // P
 PER_RANK = C // R
 GATHER_EXPERTS = 3
-FIRST_GATHER = (5, 3, 4)
+FIRST_GATHER = (1, 3, 2)
 GATHER_LEAD = 3
-RING = 7
-SCALAR_COLS = 96
+RING = 8
+SCALAR_COLS = 64
 STORE_EDGES = (0, 18, 22, 24)
 
 
@@ -72,23 +72,28 @@ def tile_moe_pke_lin_relu_kernel(tc, x_words, x_scales, w, b, offs, out):
             nc.vector.tensor_copy(picked[:], windows[table][:].indirect(offsets[:, e0 * C // 16 : e1 * C // 16]))
             slots[table].extend(picked[:, (e - e0) * C : (e - e0 + 1) * C] for e in range(e0, e1))
 
+        w_passes = w.rearrange("e (o p j) n -> p (e o) j n", p=P, j=PACK)
         rounded_of = {}
 
-        def load_and_cast(e):
-            raw = raw_pool.tile([P, PASSES, PACK, N], F32, name="raw")
-            nc.sync.dma_start(raw[:], w[e].rearrange("(o p j) n -> p o j n", p=P, j=PACK))
-            rounded = ring.tile([P, PASSES, N, PACK], BF16, name="rounded", tag="ring%d" % (e % RING), align_bytes=64)
-            rounded_of[e] = rounded
+        def cast_views(e, o, rows, n0, n1):
+            return (
+                rounded_of[e][:, o, n0:n1, :].rearrange("p (c i) j -> p c j i", i=4),
+                rows[:, :, n0:n1].rearrange("p j (c i) -> p c j i", i=4),
+            )
 
-            def views(o, n0, n1):
-                return (
-                    rounded[:, o, n0:n1, :].rearrange("p (c i) j -> p c j i", i=4),
-                    raw[:, o, :, n0:n1].rearrange("p j (c i) -> p c j i", i=4),
+        def load_and_cast(step):
+            g0, g1 = max(2 * step - 1, 0), min(2 * step + 1, E * PASSES)
+            raw = raw_pool.tile([P, g1 - g0, PACK, N], F32, name="raw")
+            nc.sync.dma_start(raw[:], w_passes[:, g0:g1])
+            if step < E:
+                rounded_of[step] = ring.tile(
+                    [P, PASSES, N, PACK], BF16, name="rounded", tag="ring%d" % (step % RING), align_bytes=64
                 )
-
-            nc.scalar.copy(*views(0, 0, N))
-            nc.scalar.copy(*views(1, 0, SCALAR_COLS))
-            nc.vector.tensor_copy(*views(1, SCALAR_COLS, N))
+                rows = raw[:, g1 - g0 - 1]
+                nc.vector.tensor_copy(*cast_views(step, 0, rows, SCALAR_COLS, N))
+                nc.scalar.copy(*cast_views(step, 0, rows, 0, SCALAR_COLS))
+            if step >= 1:
+                nc.scalar.copy(*cast_views(step - 1, 1, raw[:, 0], 0, N))
 
         def quantize(e):
             codes = code_pool.tile([P, PASSES * N], U32, name="codes", align_bytes=64)
@@ -114,6 +119,9 @@ def tile_moe_pke_lin_relu_kernel(tc, x_words, x_scales, w, b, offs, out):
                         start=(o == 0),
                         stop=(o == PASSES - 1),
                     )
+            return acc
+
+        def finish(e, acc):
             e0 = max(edge for edge in STORE_EDGES if edge <= e)
             for h in range(HALVES):
                 nc.scalar.activation(
@@ -124,17 +132,23 @@ def tile_moe_pke_lin_relu_kernel(tc, x_words, x_scales, w, b, offs, out):
                 )
 
         for table in (0, 2, 1):
-            gather(table, 0, "ring%d" % (FIRST_GATHER[table] + 1))
-        for step in range(E + 1):
-            if step < E:
+            first = FIRST_GATHER[table]
+            gather(table, 0, "ring%d" % ((first - GATHER_EXPERTS - GATHER_LEAD) % RING))
+            if first < GATHER_LEAD:
+                gather(table, first, "ring%d" % ((first - GATHER_LEAD) % RING))
+        sums = {}
+        for step in range(E + 2):
+            if step <= E:
                 load_and_cast(step)
-            if step >= 1:
+            if step >= 2:
+                finish(step - 2, sums[step - 2])
+            if 1 <= step <= E:
                 e = step - 1
                 codes, scales = quantize(e)
                 for table, edges in enumerate(gather_edges):
                     if e + GATHER_LEAD in edges[:-1]:
                         gather(table, e + GATHER_LEAD, "ring%d" % (e % RING))
-                multiply(e, codes, scales)
+                sums[e] = multiply(e, codes, scales)
 
         for e0, e1 in zip(STORE_EDGES[:-1], STORE_EDGES[1:]):
             for h in range(HALVES):

@@ -13,7 +13,8 @@ U32 = mybir.dt.uint32
 U16 = mybir.dt.uint16
 U8 = mybir.dt.uint8
 FP8X4 = mybir.dt.float8_e4m3fn_x4
-RELU = mybir.ActivationFunctionType.Relu
+ADD = mybir.AluOpType.add
+MAX = mybir.AluOpType.max
 
 P = 128
 PACK = 4
@@ -24,7 +25,7 @@ GATHER_EXPERTS = 3
 FIRST_GATHER = (1, 3, 2)
 GATHER_LEAD = 3
 RING = 8
-SCALAR_COLS = 64
+SCALAR_COLS = 160
 STORE_EDGES = (0, 18, 22, 24)
 
 
@@ -124,11 +125,13 @@ def tile_moe_pke_lin_relu_kernel(tc, x_words, x_scales, w, b, offs, out):
         def finish(e, acc):
             e0 = max(edge for edge in STORE_EDGES if edge <= e)
             for h in range(HALVES):
-                nc.scalar.activation(
+                nc.vector.tensor_scalar(
                     results[e0, h][:, :, (e - e0) * PER_RANK : (e - e0 + 1) * PER_RANK],
                     acc[:, h, :].rearrange("p (m u) -> p m u", m=R),
-                    RELU,
-                    bias=bias[:, h, e : e + 1],
+                    bias[:, h, e : e + 1],
+                    0.0,
+                    ADD,
+                    MAX,
                 )
 
         for table in (0, 2, 1):

from contextlib import ExitStack

import concourse.mybir as mybir

K, T, E, C, N = 1024, 2048, 24, 128, 256
R = 2
FLOPS = 2 * K * N * E * C

F32 = mybir.dt.float32
BF16 = mybir.dt.bfloat16
I32 = mybir.dt.int32
U32 = mybir.dt.uint32
U16 = mybir.dt.uint16
U8 = mybir.dt.uint8
FP8X4 = mybir.dt.float8_e4m3fn_x4
ADD = mybir.AluOpType.add
MAX = mybir.AluOpType.max

P = 128
PACK = 4
PASSES = K // (P * PACK)
HALVES = N // P
PER_RANK = C // R
GATHER_EXPERTS = 3
FIRST_GATHER = (1, 3, 2)
GATHER_LEAD = 3
RING = 8
SCALAR_COLS = 160
STORE_EDGES = (0, 18, 22, 24)


def tile_moe_pke_lin_relu_kernel(tc, x_words, x_scales, w, b, offs, out):
    nc = tc.nc
    with ExitStack() as ctx:
        keep = ctx.enter_context(tc.tile_pool(name="keep", bufs=1))
        raw_pool = ctx.enter_context(tc.tile_pool(name="raw", bufs=12))
        ring = ctx.enter_context(tc.tile_pool(name="ring", bufs=1))
        code_pool = ctx.enter_context(tc.tile_pool(name="code", bufs=4))
        psum = ctx.enter_context(tc.psum_pool(name="psum", bufs=4))

        offsets = keep.tile([P, E * C // 16], U16, name="offsets")
        nc.sync.dma_start(offsets[:], offs)

        scale_rows = keep.tile([P, T // 4], I32, name="scale_rows")
        token_scales = keep.tile([P, T], U8, name="token_scales", align_bytes=64)
        nc.vector.memset(token_scales[:].bitcast(I32), 0)
        for q in range(4):
            live = slice(32 * q, 32 * q + 4 * PASSES)
            nc.sync.dma_start(scale_rows[live, :], x_scales[:, 4 * q : 4 * q + 4, :].bitcast(I32))
            nc.vector.tensor_copy(token_scales[live, :].bitcast(I32), scale_rows[live, :])
        token_words = []
        for o in range(PASSES):
            words = keep.tile([P, T], U32, name="token_words%d" % o, align_bytes=64)
            nc.sync.dma_start(words[:].bitcast(I32), x_words[o].rearrange("p t r -> p (t r)").bitcast(I32))
            token_words.append(words)
        bias = keep.tile([P, HALVES, E], F32, name="bias")
        nc.sync.dma_start(bias[:], b.rearrange("(h p) e -> p h e", p=P))

        results = {}
        for e0, e1 in zip(STORE_EDGES[:-1], STORE_EDGES[1:]):
            for h in range(HALVES):
                results[e0, h] = keep.tile([P, R, (e1 - e0) * PER_RANK], F32, name="result%d_%d" % (e0, h))

        windows = token_words + [token_scales]
        gather_edges = [[0] + list(range(first, E - 1, GATHER_EXPERTS)) + [E] for first in FIRST_GATHER]
        slots = [[] for window in windows]

        def gather(table, e0, tag):
            edges = gather_edges[table]
            e1 = edges[edges.index(e0) + 1]
            dtype = U8 if table == PASSES else U32
            picked = ring.tile([P, (e1 - e0) * C], dtype, name="picked", tag=tag, align_bytes=64)
            nc.vector.tensor_copy(picked[:], windows[table][:].indirect(offsets[:, e0 * C // 16 : e1 * C // 16]))
            slots[table].extend(picked[:, (e - e0) * C : (e - e0 + 1) * C] for e in range(e0, e1))

        w_passes = w.rearrange("e (o p j) n -> p (e o) j n", p=P, j=PACK)
        rounded_of = {}

        def cast_views(e, o, rows, n0, n1):
            return (
                rounded_of[e][:, o, n0:n1, :].rearrange("p (c i) j -> p c j i", i=4),
                rows[:, :, n0:n1].rearrange("p j (c i) -> p c j i", i=4),
            )

        def load_and_cast(step):
            g0, g1 = max(2 * step - 1, 0), min(2 * step + 1, E * PASSES)
            raw = raw_pool.tile([P, g1 - g0, PACK, N], F32, name="raw")
            nc.sync.dma_start(raw[:], w_passes[:, g0:g1])
            if step < E:
                rounded_of[step] = ring.tile(
                    [P, PASSES, N, PACK], BF16, name="rounded", tag="ring%d" % (step % RING), align_bytes=64
                )
                rows = raw[:, g1 - g0 - 1]
                nc.vector.tensor_copy(*cast_views(step, 0, rows, SCALAR_COLS, N))
                nc.scalar.copy(*cast_views(step, 0, rows, 0, SCALAR_COLS))
            if step >= 1:
                nc.scalar.copy(*cast_views(step - 1, 1, raw[:, 0], 0, N))

        def quantize(e):
            codes = code_pool.tile([P, PASSES * N], U32, name="codes", align_bytes=64)
            scales = code_pool.tile([P, PASSES * N], U8, name="scales", align_bytes=64)
            nc.vector.quantize_mx(
                out=codes[:].bitcast(FP8X4),
                scales=scales[:],
                in_=rounded_of[e][:].rearrange("p o n j -> p (o n j)"),
            )
            return codes, scales

        def multiply(e, codes, scales):
            acc = psum.tile([P, HALVES, C], F32, name="acc")
            for h in range(HALVES):
                for o in range(PASSES):
                    cols = slice(o * N + h * P, o * N + (h + 1) * P)
                    nc.tensor.matmul_mx(
                        out=acc[:, h, :],
                        lhsT=codes[:, cols].bitcast(FP8X4),
                        lhsT_scale=scales[:, cols],
                        rhs=slots[o][e].bitcast(FP8X4),
                        rhs_scale=slots[PASSES][e][4 * o : P, :],
                        start=(o == 0),
                        stop=(o == PASSES - 1),
                    )
            return acc

        def finish(e, acc):
            e0 = max(edge for edge in STORE_EDGES if edge <= e)
            for h in range(HALVES):
                nc.vector.tensor_scalar(
                    results[e0, h][:, :, (e - e0) * PER_RANK : (e - e0 + 1) * PER_RANK],
                    acc[:, h, :].rearrange("p (m u) -> p m u", m=R),
                    bias[:, h, e : e + 1],
                    0.0,
                    ADD,
                    MAX,
                )

        for table in (0, 2, 1):
            first = FIRST_GATHER[table]
            gather(table, 0, "ring%d" % ((first - GATHER_EXPERTS - GATHER_LEAD) % RING))
            if first < GATHER_LEAD:
                gather(table, first, "ring%d" % ((first - GATHER_LEAD) % RING))
        sums = {}
        for step in range(E + 2):
            if step <= E:
                load_and_cast(step)
            if step >= 2:
                finish(step - 2, sums[step - 2])
            if 1 <= step <= E:
                e = step - 1
                codes, scales = quantize(e)
                for table, edges in enumerate(gather_edges):
                    if e + GATHER_LEAD in edges[:-1]:
                        gather(table, e + GATHER_LEAD, "ring%d" % (e % RING))
                sums[e] = multiply(e, codes, scales)

        for e0, e1 in zip(STORE_EDGES[:-1], STORE_EDGES[1:]):
            for h in range(HALVES):
                rows = out[h * P : (h + 1) * P, :].rearrange("p (m c) -> p m c", m=R)
                nc.sync.dma_start(rows[:, :, e0 * PER_RANK : e1 * PER_RANK], results[e0, h][:])
